import numpy as np
import ml_dtypes


def mxq(x, axis, fmt="e4m3"):
    dtype, down = {"e4m3": (ml_dtypes.float8_e4m3fn, 7), "e5m2": (ml_dtypes.float8_e5m2, 14)}[fmt]
    v = np.moveaxis(np.asarray(x, np.float32).astype(ml_dtypes.bfloat16).astype(np.float64), axis, -1)
    blocks = v.reshape(v.shape[:-1] + (-1, 32))
    amax = np.abs(blocks).max(-1, keepdims=True)
    byte = np.maximum(np.where(amax > 0, np.frexp(amax)[1] - 1 + 127, 0) - down, 1)
    scale = np.exp2(byte - 127.0)
    codes = (blocks / scale).astype(np.float32).astype(dtype).astype(np.float64)
    return np.moveaxis((codes * scale).reshape(v.shape), -1, axis)


WIDE = False


def mx_kscale(k):
    if not WIDE:
        return np.ones(k)
    levels = np.array([30, -30])
    if k % 512:
        return np.exp2(np.random.permutation(np.resize(levels, k // 32))).repeat(32)
    a = np.empty((k // 512, 16))
    for p in range(k // 512):
        a[p, :8] = np.random.permutation(np.resize(levels, 8))
        for g in range(8):
            far = levels[np.abs(levels - a[p, g]) >= 10]
            a[p, g + 8] = far[np.random.randint(len(far))]
    return np.exp2(a.ravel()).repeat(32)


def f64(x):
    return np.asarray(x).astype(np.float64)


E2M1 = np.array([0.0, 0.5, 1.0, 1.5, 2.0, 3.0, 4.0, 6.0, -0.0, -0.5, -1.0, -1.5, -2.0, -3.0, -4.0, -6.0])


def pack_weight(w, fmt):
    k, n = w.shape
    w = f64(np.asarray(w, np.float32).astype(ml_dtypes.bfloat16)).reshape(k // 32, 32, n)
    amax = np.abs(w).max(1)
    if fmt == "e4m3":
        byte = np.frexp(amax)[1] - 1 + 127 - 7
    else:
        mant, ex = np.frexp(amax / 6.0)
        byte = np.where(mant > 0.5, ex, ex - 1) + 127
    byte = np.clip(np.where(amax > 0, byte, 1), 1, 254)
    scaled = (w * np.exp2(127.0 - byte)[:, None, :]).reshape(k, n).astype(np.float32)
    by_word = np.ascontiguousarray(scaled.reshape(k // 512, 128, 4, n).transpose(0, 1, 3, 2))
    if fmt == "e4m3":
        words = by_word.astype(ml_dtypes.float8_e4m3fn).view(np.uint8)
    else:
        c = by_word.astype(ml_dtypes.float4_e2m1fn).view(np.uint8) & 0xF
        words = (c[..., 0::2] | (c[..., 1::2] << 4)).reshape(k // 512, 128, 2 * n)
    return np.ascontiguousarray(words), np.ascontiguousarray(byte.astype(np.uint8).reshape(k // 512, 16, n))


def unpack_weight(words, scales, fmt):
    g, _, n = scales.shape
    words = np.ascontiguousarray(words).reshape(g, 128, n, -1)
    if fmt == "e4m3":
        vals = words.view(ml_dtypes.float8_e4m3fn).astype(np.float64)
    else:
        nib = np.empty((g, 128, n, 4), np.uint8)
        nib[..., 0::2] = words & 0xF
        nib[..., 1::2] = words >> 4
        vals = E2M1[nib]
    vals = vals * np.repeat(np.exp2(scales.astype(np.float64) - 127.0), 8, axis=1)[..., None]
    return vals.transpose(0, 1, 3, 2).reshape(g * 512, n)


def bf(x):
    return np.asarray(x, np.float32).astype(ml_dtypes.bfloat16)


def planes(Y):
    r, m = Y.shape
    b = f64(bf(Y)).reshape(r // 32, 32, m)
    amax = np.abs(b).max(1)
    byte = np.clip(np.where(amax > 0, np.frexp(amax)[1] - 1 + 127 - 7, 1), 1, 254)
    codes = (b * np.exp2(127.0 - byte)[:, None, :]).reshape(r, m).astype(np.float32).astype(ml_dtypes.float8_e4m3fn).view(np.uint8)
    words = codes.reshape(r // 512, 128, 4, m).transpose(0, 1, 3, 2)
    return np.ascontiguousarray(words), np.ascontiguousarray(byte.astype(np.uint8).reshape(r // 512, 16, m))


T, S, K, N = 1024, 1024, 512, 512


def setup_inputs():
    n = np.random.standard_normal
    ft = mx_kscale(T)
    fs = mx_kscale(S)
    xsp = pack_weight(n((S, K)) * fs[:, None], "e2m1")
    gsp = pack_weight(n((S, N)) / fs[:, None], "e4m3")
    return {
        "xa": (n((T, K)) * ft[:, None]).astype(np.float32),
        "ga": (n((T, N)) * np.exp(0.5 * n((T, 1))) / ft[:, None]).astype(np.float32),
        "xs_words": xsp[0],
        "xs_scales": xsp[1],
        "gs_words": gsp[0],
        "gs_scales": gsp[1],
        "mom": (1.0 * n((K, N))).astype(np.float32),
    }


def reference(xa, ga, xs_words, xs_scales, gs_words, gs_scales, mom):
    xsu = unpack_weight(xs_words, xs_scales, "e2m1")
    gsu = unpack_weight(gs_words, gs_scales, "e4m3")
    xaq = mxq(f64(xa), 0, "e4m3")
    gaq = mxq(f64(ga), 0, "e5m2")
    w = xaq.T @ gaq + xsu.T @ gsu
    y = 0.02 * w + 0.5 * f64(mom)
    words, scales = planes(y)
    return y, words, scales

@@ -1,0 +1,190 @@
+from contextlib import ExitStack
+
+import concourse.mybir as mybir
+
+T, S, K, N = 1024, 1024, 512, 512
+FLOPS = 2 * (T + S) * K * N
+
+F32 = mybir.dt.float32
+BF16 = mybir.dt.bfloat16
+I32 = mybir.dt.int32
+U32 = mybir.dt.uint32
+U8 = mybir.dt.uint8
+E4M3 = mybir.dt.float8_e4m3fn_x4
+E5M2 = mybir.dt.float8_e5m2_x4
+E2M1 = mybir.dt.float4_e2m1fn_x4
+ALU = mybir.AluOpType
+COPY = mybir.ActivationFunctionType.Copy
+
+P = 128
+PACK = 4
+PASS = P * PACK
+
+
+def tile_mix_wgrad_of_two_stores_pl_kernel(tc, xa, ga, xs_words, xs_scales, gs_words, gs_scales, mom, out_0, out_1, out_2):
+    nc = tc.nc
+    with ExitStack() as ctx:
+        sb = ctx.enter_context(tc.tile_pool(name="sb", bufs=1))
+        psum = ctx.enter_context(tc.psum_pool(name="psum", bufs=1))
+        ctx.enter_context(tc.manual_schedule())
+
+        def tile(name, shape, dtype):
+            return sb.tile(shape, dtype, name=name, align_bytes=64)
+
+        acc = [psum.tile([P, N], F32, name="acc%d" % r) for r in range(PACK)]
+
+        xs_raw = tile("xs_raw", [P, 2048], U8)
+        xs_sc_raw = tile("xs_sc_raw", [P, 1024], U8)
+        xs_dealt = tile("xs_dealt", [P, 2048], U8)
+        xs_sc = tile("xs_sc", [P, 1024], U8)
+        gs_codes = tile("gs_codes", [P, 2 * N], U32)
+        gs_sc = tile("gs_sc", [P, 2 * N], U8)
+
+        def load_scales(plane, scales, q):
+            nc.sync.dma_start(
+                out=plane[32 * q : 32 * q + 4, :].bitcast(I32).rearrange("p (z c) -> p z c", z=2),
+                in_=scales[:, 4 * q : 4 * q + 4, :].rearrange("z r c -> r z c").bitcast(I32),
+            )
+
+        def load_rows(name, src, a, c0, c1):
+            raw = tile(name, [P, PACK, c1 - c0], F32)
+            nc.sync.dma_start(out=raw[:], in_=src[PASS * a : PASS * (a + 1), c0:c1].rearrange("(p j) w -> p j w", j=PACK))
+            return raw
+
+        nc.vector.memset(xs_sc_raw[:].bitcast(I32), 0)
+        nc.vector.memset(gs_sc[:].bitcast(I32), 0)
+
+        ga_cuts = [(0, 0, 256), (0, 256, 512), (1, 0, 256), (1, 256, 384), (1, 384, 512)]
+        nc.sync.dma_start(
+            out=xs_raw[:].bitcast(I32).rearrange("p (z w) -> p z w", z=2),
+            in_=xs_words.rearrange("z p b -> p z b").bitcast(I32),
+        )
+        xa_raw = {}
+        xa_raw[0, 0] = load_rows("xa00", xa, 0, 0, 256)
+        for q in range(4):
+            load_scales(xs_sc_raw, xs_scales, q)
+        xa_raw[0, 1] = load_rows("xa01", xa, 0, 256, 512)
+        xa_raw[1, 0] = load_rows("xa10", xa, 1, 0, 256)
+        xa_raw[1, 1] = load_rows("xa11", xa, 1, 256, 512)
+        for q in range(4):
+            load_scales(gs_sc, gs_scales, q)
+        nc.sync.dma_start(
+            out=gs_codes[:].bitcast(I32).rearrange("p (z n) -> p z n", z=2),
+            in_=gs_words.rearrange("z p n t -> p z (n t)").bitcast(I32),
+        )
+        ga_raw = [load_rows("ga%d" % i, ga, a, c0, c1) for i, (a, c0, c1) in enumerate(ga_cuts)]
+        mom_v = mom.rearrange("(p r) n -> p r n", r=PACK)
+        out_v = out_0.rearrange("(p r) n -> p r n", r=PACK)
+        pieces = [(0, 1, 0, 512), (1, 2, 0, 512), (2, 4, 0, 256), (2, 4, 256, 512)]
+        mom_raw = []
+        for i, (r0, r1, c0, c1) in enumerate(pieces):
+            m = tile("mom%d" % i, [P, r1 - r0, c1 - c0], F32)
+            nc.sync.dma_start(out=m[:], in_=mom_v[:, r0:r1, c0:c1])
+            mom_raw.append(m)
+
+        nc.vector.tensor_copy(
+            out=xs_dealt[:].rearrange("p (r g m b) -> p g r m b", r=4, m=8, b=2),
+            in_=xs_raw[:].rearrange("p (g m r b) -> p g r m b", r=4, m=8, b=2),
+        )
+        nc.vector.tensor_copy(
+            out=xs_sc[:].rearrange("p (r g m) -> p g r m", r=4, m=16),
+            in_=xs_sc_raw[:].rearrange("p (g m r) -> p g r m", r=4, m=16),
+        )
+
+        xa_codes = [tile("xa_codes%d" % a, [P, K], U32) for a in range(2)]
+        xa_sc = [tile("xa_sc%d" % a, [P, K], U8) for a in range(2)]
+        for a in range(2):
+            xa_bf = tile("xa_bf%d" % a, [P, PACK * K], BF16)
+            for h in range(2):
+                nc.scalar.activation(
+                    out=xa_bf[:].rearrange("p (r m j) -> p m j r", r=4, j=4)[:, 64 * h : 64 * (h + 1)],
+                    in_=xa_raw[a, h][:].rearrange("p j (m r) -> p m j r", r=4),
+                    func=COPY,
+                )
+            nc.vector.quantize_mx(out=xa_codes[a][:].bitcast(E4M3), scales=xa_sc[a][:], in_=xa_bf[:])
+
+        for z in range(2):
+            for r in range(PACK):
+                col = 2 * r + z
+                nc.tensor.matmul_mx(
+                    out=acc[r][:],
+                    lhsT=xs_dealt[:, 256 * col : 256 * (col + 1)].bitcast(E2M1),
+                    lhsT_scale=xs_sc[:, 128 * col : 128 * (col + 1)],
+                    rhs=gs_codes[:, N * z : N * (z + 1)].bitcast(E4M3),
+                    rhs_scale=gs_sc[:, N * z : N * (z + 1)],
+                    start=(z == 0),
+                    stop=False,
+                )
+
+        ga_codes = [tile("ga_codes%d" % a, [P, N], U32) for a in range(2)]
+        ga_sc = [tile("ga_sc%d" % a, [P, N], U8) for a in range(2)]
+        ga_bf = [tile("ga_bf%d" % i, [P, PACK * (c1 - c0)], BF16) for i, (a, c0, c1) in enumerate(ga_cuts)]
+
+        def round_ga(i, on_scalar):
+            dst = ga_bf[i][:].rearrange("p (c i j) -> p c j i", i=4, j=4)
+            src = ga_raw[i][:].rearrange("p j (c i) -> p c j i", i=4)
+            if on_scalar:
+                nc.scalar.activation(out=dst, in_=src, func=COPY)
+            else:
+                nc.vector.tensor_copy(out=dst, in_=src)
+
+        def quant_ga(i):
+            a, c0, c1 = ga_cuts[i]
+            nc.vector.quantize_mx(out=ga_codes[a][:, c0:c1].bitcast(E5M2), scales=ga_sc[a][:, c0:c1], in_=ga_bf[i][:])
+
+        def fresh_pass(a):
+            for r in range(PACK):
+                nc.tensor.matmul_mx(
+                    out=acc[r][:],
+                    lhsT=xa_codes[a][:, P * r : P * (r + 1)].bitcast(E4M3),
+                    lhsT_scale=xa_sc[a][:, P * r : P * (r + 1)],
+                    rhs=ga_codes[a][:].bitcast(E5M2),
+                    rhs_scale=ga_sc[a][:],
+                    start=False,
+                    stop=(a == 1),
+                )
+
+        round_ga(0, True)
+        round_ga(1, False)
+        quant_ga(0)
+        quant_ga(1)
+        fresh_pass(0)
+        round_ga(2, False)
+        round_ga(3, True)
+        quant_ga(2)
+        round_ga(4, False)
+        quant_ga(3)
+        quant_ga(4)
+        fresh_pass(1)
+
+        y = []
+        for i, (r0, r1, c0, c1) in enumerate(pieces):
+            half = tile("half%d" % i, [P, r1 - r0, c1 - c0], F32)
+            nc.scalar.activation(out=half[:], in_=mom_raw[i][:], func=COPY, scale=0.5)
+            y.append(half)
+        ysb = tile("ysb", [P, PACK, N], F32)
+        for i, (r0, r1, c0, c1) in enumerate(pieces):
+            for r in range(r0, r1):
+                nc.vector.scalar_tensor_tensor(
+                    out=ysb[:, r, c0:c1], in0=acc[r][:, c0:c1], scalar=0.02, in1=y[i][:, r - r0, :], op0=ALU.mult, op1=ALU.add
+                )
+            nc.sync.dma_start(out=out_v[:, r0:r1, c0:c1], in_=ysb[:, r0:r1, c0:c1])
+
+        y_codes = tile("y_codes", [P, N], U32)
+        y_sc = tile("y_sc", [P, N], U8)
+        y_bf = [tile("y_bf%d" % h, [P, PACK * 256], BF16) for h in range(2)]
+        for h in range(2):
+            dst = y_bf[h][:].rearrange("p (c i r) -> p c r i", i=4, r=4)
+            src = ysb[:, :, 256 * h : 256 * (h + 1)].rearrange("p r (c i) -> p c r i", i=4)
+            if h == 0:
+                nc.scalar.activation(out=dst, in_=src, func=COPY)
+            else:
+                nc.vector.tensor_copy(out=dst, in_=src)
+        words_v = out_1[0].rearrange("p c r -> p (c r)").bitcast(I32)
+        for h in range(2):
+            cols = slice(256 * h, 256 * (h + 1))
+            nc.vector.quantize_mx(out=y_codes[:, cols].bitcast(E4M3), scales=y_sc[:, cols], in_=y_bf[h][:])
+        nc.sync.dma_start(out=words_v, in_=y_codes[:].bitcast(I32))
+        for q in range(4):
+            queue = nc.sync if q < 2 else nc.scalar
+            queue.dma_start(out=out_2[0, 4 * q : 4 * q + 4, :].bitcast(I32), in_=y_sc[32 * q : 32 * q + 4, :].bitcast(I32))

@@ -37,7 +37,7 @@ def tile_mix_wgrad_of_two_stores_pl_kernel(tc, xa, ga, xs_words, xs_scales, gs_w
         xs_sc_raw = tile("xs_sc_raw", [P, 1024], U8)
         xs_dealt = tile("xs_dealt", [P, 2048], U8)
         xs_sc = tile("xs_sc", [P, 1024], U8)
-        gs_codes = tile("gs_codes", [P, 2 * N], U32)
+        gs_codes = [tile("gs_codes%d" % z, [P, N], U32) for z in range(2)]
         gs_sc = tile("gs_sc", [P, 2 * N], U8)
 
         def load_scales(plane, scales, q):
@@ -54,25 +54,21 @@ def tile_mix_wgrad_of_two_stores_pl_kernel(tc, xa, ga, xs_words, xs_scales, gs_w
         nc.vector.memset(xs_sc_raw[:].bitcast(I32), 0)
         nc.vector.memset(gs_sc[:].bitcast(I32), 0)
 
-        ga_cuts = [(0, 0, 256), (0, 256, 512), (1, 0, 256), (1, 256, 384), (1, 384, 512)]
+        ga_cuts = [(0, 0, 512), (1, 0, 256), (1, 256, 512)]
+        gs_v = gs_words.rearrange("z p n t -> z p (n t)").bitcast(I32)
         nc.sync.dma_start(
             out=xs_raw[:].bitcast(I32).rearrange("p (z w) -> p z w", z=2),
             in_=xs_words.rearrange("z p b -> p z b").bitcast(I32),
         )
-        xa_raw = {}
-        xa_raw[0, 0] = load_rows("xa00", xa, 0, 0, 256)
+        xa_raw = [load_rows("xa0", xa, 0, 0, 512)]
         for q in range(4):
             load_scales(xs_sc_raw, xs_scales, q)
-        xa_raw[0, 1] = load_rows("xa01", xa, 0, 256, 512)
-        xa_raw[1, 0] = load_rows("xa10", xa, 1, 0, 256)
-        xa_raw[1, 1] = load_rows("xa11", xa, 1, 256, 512)
+        xa_raw.append(load_rows("xa1", xa, 1, 0, 512))
         for q in range(4):
             load_scales(gs_sc, gs_scales, q)
-        nc.sync.dma_start(
-            out=gs_codes[:].bitcast(I32).rearrange("p (z n) -> p z n", z=2),
-            in_=gs_words.rearrange("z p n t -> p z (n t)").bitcast(I32),
-        )
+        nc.sync.dma_start(out=gs_codes[0][:].bitcast(I32), in_=gs_v[0])
         ga_raw = [load_rows("ga%d" % i, ga, a, c0, c1) for i, (a, c0, c1) in enumerate(ga_cuts)]
+        nc.sync.dma_start(out=gs_codes[1][:].bitcast(I32), in_=gs_v[1])
         mom_v = mom.rearrange("(p r) n -> p r n", r=PACK)
         out_v = out_0.rearrange("(p r) n -> p r n", r=PACK)
         pieces = [(0, 1, 0, 512), (1, 2, 0, 512), (2, 4, 0, 256), (2, 4, 256, 512)]
@@ -94,68 +90,73 @@ def tile_mix_wgrad_of_two_stores_pl_kernel(tc, xa, ga, xs_words, xs_scales, gs_w
         xa_codes = [tile("xa_codes%d" % a, [P, K], U32) for a in range(2)]
         xa_sc = [tile("xa_sc%d" % a, [P, K], U8) for a in range(2)]
         for a in range(2):
-            xa_bf = tile("xa_bf%d" % a, [P, PACK * K], BF16)
+            xa_bf = [tile("xa_bf%d%d" % (a, h), [P, 2 * K], BF16) for h in range(2)]
+            src = xa_raw[a][:].rearrange("p j (m r) -> p m j r", r=4)
+            nc.vector.tensor_copy(out=xa_bf[0][:].rearrange("p (r m j) -> p m j r", r=2, j=4), in_=src[:, :, :, 0:2])
+            nc.scalar.activation(out=xa_bf[1][:].rearrange("p (r m j) -> p m j r", r=2, j=4), in_=src[:, :, :, 2:4], func=COPY)
             for h in range(2):
-                nc.scalar.activation(
-                    out=xa_bf[:].rearrange("p (r m j) -> p m j r", r=4, j=4)[:, 64 * h : 64 * (h + 1)],
-                    in_=xa_raw[a, h][:].rearrange("p j (m r) -> p m j r", r=4),
-                    func=COPY,
-                )
-            nc.vector.quantize_mx(out=xa_codes[a][:].bitcast(E4M3), scales=xa_sc[a][:], in_=xa_bf[:])
+                cols = slice(256 * h, 256 * (h + 1))
+                nc.vector.quantize_mx(out=xa_codes[a][:, cols].bitcast(E4M3), scales=xa_sc[a][:, cols], in_=xa_bf[h][:])
 
-        for z in range(2):
-            for r in range(PACK):
-                col = 2 * r + z
-                nc.tensor.matmul_mx(
-                    out=acc[r][:],
-                    lhsT=xs_dealt[:, 256 * col : 256 * (col + 1)].bitcast(E2M1),
-                    lhsT_scale=xs_sc[:, 128 * col : 128 * (col + 1)],
-                    rhs=gs_codes[:, N * z : N * (z + 1)].bitcast(E4M3),
-                    rhs_scale=gs_sc[:, N * z : N * (z + 1)],
-                    start=(z == 0),
-                    stop=False,
-                )
+        def stored_mm(z, r):
+            col = 2 * r + z
+            nc.tensor.matmul_mx(
+                out=acc[r][:],
+                lhsT=xs_dealt[:, 256 * col : 256 * (col + 1)].bitcast(E2M1),
+                lhsT_scale=xs_sc[:, 128 * col : 128 * (col + 1)],
+                rhs=gs_codes[z][:].bitcast(E4M3),
+                rhs_scale=gs_sc[:, N * z : N * (z + 1)],
+                start=(z == 0),
+                stop=False,
+            )
+
+        def fresh_mm(a, r):
+            nc.tensor.matmul_mx(
+                out=acc[r][:],
+                lhsT=xa_codes[a][:, P * r : P * (r + 1)].bitcast(E4M3),
+                lhsT_scale=xa_sc[a][:, P * r : P * (r + 1)],
+                rhs=ga_codes[a][:].bitcast(E5M2),
+                rhs_scale=ga_sc[a][:],
+                start=False,
+                stop=(a == 1),
+            )
 
         ga_codes = [tile("ga_codes%d" % a, [P, N], U32) for a in range(2)]
         ga_sc = [tile("ga_sc%d" % a, [P, N], U8) for a in range(2)]
         ga_bf = [tile("ga_bf%d" % i, [P, PACK * (c1 - c0)], BF16) for i, (a, c0, c1) in enumerate(ga_cuts)]
 
-        def round_ga(i, on_scalar):
-            dst = ga_bf[i][:].rearrange("p (c i j) -> p c j i", i=4, j=4)
-            src = ga_raw[i][:].rearrange("p j (c i) -> p c j i", i=4)
+        def round_ga(i, c0, c1, on_scalar):
+            dst = ga_bf[i][:, PACK * c0 : PACK * c1].rearrange("p (c i j) -> p c j i", i=4, j=4)
+            src = ga_raw[i][:, :, c0:c1].rearrange("p j (c i) -> p c j i", i=4)
             if on_scalar:
                 nc.scalar.activation(out=dst, in_=src, func=COPY)
             else:
                 nc.vector.tensor_copy(out=dst, in_=src)
 
-        def quant_ga(i):
-            a, c0, c1 = ga_cuts[i]
-            nc.vector.quantize_mx(out=ga_codes[a][:, c0:c1].bitcast(E5M2), scales=ga_sc[a][:, c0:c1], in_=ga_bf[i][:])
+        def quant_ga(i, c0, c1):
+            a, base, end = ga_cuts[i]
+            nc.vector.quantize_mx(
+                out=ga_codes[a][:, base + c0 : base + c1].bitcast(E5M2),
+                scales=ga_sc[a][:, base + c0 : base + c1],
+                in_=ga_bf[i][:, PACK * c0 : PACK * c1],
+            )
 
-        def fresh_pass(a):
-            for r in range(PACK):
-                nc.tensor.matmul_mx(
-                    out=acc[r][:],
-                    lhsT=xa_codes[a][:, P * r : P * (r + 1)].bitcast(E4M3),
-                    lhsT_scale=xa_sc[a][:, P * r : P * (r + 1)],
-                    rhs=ga_codes[a][:].bitcast(E5M2),
-                    rhs_scale=ga_sc[a][:],
-                    start=False,
-                    stop=(a == 1),
-                )
-
-        round_ga(0, True)
-        round_ga(1, False)
-        quant_ga(0)
-        quant_ga(1)
-        fresh_pass(0)
-        round_ga(2, False)
-        round_ga(3, True)
-        quant_ga(2)
-        round_ga(4, False)
-        quant_ga(3)
-        quant_ga(4)
-        fresh_pass(1)
+        for r in range(PACK):
+            stored_mm(0, r)
+        round_ga(0, 0, 256, False)
+        round_ga(0, 256, 512, True)
+        quant_ga(0, 0, 256)
+        quant_ga(0, 256, 512)
+        for r in range(PACK):
+            fresh_mm(0, r)
+        round_ga(1, 0, 256, True)
+        round_ga(2, 0, 160, False)
+        round_ga(2, 160, 256, True)
+        quant_ga(1, 0, 256)
+        quant_ga(2, 0, 256)
+        for r in range(PACK):
+            stored_mm(1, r)
+            fresh_mm(1, r)
 
         y = []
         for i, (r0, r1, c0, c1) in enumerate(pieces):
@@ -184,7 +185,7 @@ def tile_mix_wgrad_of_two_stores_pl_kernel(tc, xa, ga, xs_words, xs_scales, gs_w
         for h in range(2):
             cols = slice(256 * h, 256 * (h + 1))
             nc.vector.quantize_mx(out=y_codes[:, cols].bitcast(E4M3), scales=y_sc[:, cols], in_=y_bf[h][:])
-        nc.sync.dma_start(out=words_v, in_=y_codes[:].bitcast(I32))
+            nc.sync.dma_start(out=words_v[:, cols], in_=y_codes[:, cols].bitcast(I32))
         for q in range(4):
-            queue = nc.sync if q < 2 else nc.scalar
+            queue = nc.sync if q < 1 else nc.scalar
             queue.dma_start(out=out_2[0, 4 * q : 4 * q + 4, :].bitcast(I32), in_=y_sc[32 * q : 32 * q + 4, :].bitcast(I32))

@@ -40,8 +40,8 @@ def tile_mix_wgrad_of_two_stores_pl_kernel(tc, xa, ga, xs_words, xs_scales, gs_w
         gs_codes = [tile("gs_codes%d" % z, [P, N], U32) for z in range(2)]
         gs_sc = tile("gs_sc", [P, 2 * N], U8)
 
-        def load_scales(plane, scales, q):
-            nc.sync.dma_start(
+        def load_scales(queue, plane, scales, q):
+            queue.dma_start(
                 out=plane[32 * q : 32 * q + 4, :].bitcast(I32).rearrange("p (z c) -> p z c", z=2),
                 in_=scales[:, 4 * q : 4 * q + 4, :].rearrange("z r c -> r z c").bitcast(I32),
             )
@@ -52,7 +52,7 @@ def tile_mix_wgrad_of_two_stores_pl_kernel(tc, xa, ga, xs_words, xs_scales, gs_w
             return raw
 
         nc.vector.memset(xs_sc_raw[:].bitcast(I32), 0)
-        nc.vector.memset(gs_sc[:].bitcast(I32), 0)
+        nc.gpsimd.memset(gs_sc[:].bitcast(I32), 0)
 
         ga_cuts = [(0, 0, 512), (1, 0, 256), (1, 256, 512)]
         gs_v = gs_words.rearrange("z p n t -> z p (n t)").bitcast(I32)
@@ -62,12 +62,14 @@ def tile_mix_wgrad_of_two_stores_pl_kernel(tc, xa, ga, xs_words, xs_scales, gs_w
         )
         xa_raw = [load_rows("xa0", xa, 0, 0, 512)]
         for q in range(4):
-            load_scales(xs_sc_raw, xs_scales, q)
-        xa_raw.append(load_rows("xa1", xa, 1, 0, 512))
+            load_scales(nc.sync, xs_sc_raw, xs_scales, q)
+        ga_raw = [load_rows("ga0", ga, 0, 0, 512)]
         for q in range(4):
-            load_scales(gs_sc, gs_scales, q)
+            load_scales(nc.gpsimd, gs_sc, gs_scales, q)
+        xa_raw.append(load_rows("xa1", xa, 1, 0, 512))
         nc.sync.dma_start(out=gs_codes[0][:].bitcast(I32), in_=gs_v[0])
-        ga_raw = [load_rows("ga%d" % i, ga, a, c0, c1) for i, (a, c0, c1) in enumerate(ga_cuts)]
+        ga_raw.append(load_rows("ga1", ga, 1, 0, 256))
+        ga_raw.append(load_rows("ga2", ga, 1, 256, 512))
         nc.sync.dma_start(out=gs_codes[1][:].bitcast(I32), in_=gs_v[1])
         mom_v = mom.rearrange("(p r) n -> p r n", r=PACK)
         out_v = out_0.rearrange("(p r) n -> p r n", r=PACK)
@@ -89,7 +91,7 @@ def tile_mix_wgrad_of_two_stores_pl_kernel(tc, xa, ga, xs_words, xs_scales, gs_w
 
         xa_codes = [tile("xa_codes%d" % a, [P, K], U32) for a in range(2)]
         xa_sc = [tile("xa_sc%d" % a, [P, K], U8) for a in range(2)]
-        for a in range(2):
+        def fresh_xa(a):
             xa_bf = [tile("xa_bf%d%d" % (a, h), [P, 2 * K], BF16) for h in range(2)]
             src = xa_raw[a][:].rearrange("p j (m r) -> p m j r", r=4)
             nc.vector.tensor_copy(out=xa_bf[0][:].rearrange("p (r m j) -> p m j r", r=2, j=4), in_=src[:, :, :, 0:2])
@@ -106,7 +108,7 @@ def tile_mix_wgrad_of_two_stores_pl_kernel(tc, xa, ga, xs_words, xs_scales, gs_w
                 lhsT_scale=xs_sc[:, 128 * col : 128 * (col + 1)],
                 rhs=gs_codes[z][:].bitcast(E4M3),
                 rhs_scale=gs_sc[:, N * z : N * (z + 1)],
-                start=(z == 0),
+                start=False,
                 stop=False,
             )
 
@@ -117,7 +119,7 @@ def tile_mix_wgrad_of_two_stores_pl_kernel(tc, xa, ga, xs_words, xs_scales, gs_w
                 lhsT_scale=xa_sc[a][:, P * r : P * (r + 1)],
                 rhs=ga_codes[a][:].bitcast(E5M2),
                 rhs_scale=ga_sc[a][:],
-                start=False,
+                start=(a == 0),
                 stop=(a == 1),
             )
 
@@ -141,22 +143,26 @@ def tile_mix_wgrad_of_two_stores_pl_kernel(tc, xa, ga, xs_words, xs_scales, gs_w
                 in_=ga_bf[i][:, PACK * c0 : PACK * c1],
             )
 
-        for r in range(PACK):
-            stored_mm(0, r)
+        fresh_xa(0)
         round_ga(0, 0, 256, False)
         round_ga(0, 256, 512, True)
         quant_ga(0, 0, 256)
         quant_ga(0, 256, 512)
         for r in range(PACK):
             fresh_mm(0, r)
+        for r in range(PACK):
+            stored_mm(0, r)
+        fresh_xa(1)
         round_ga(1, 0, 256, True)
         round_ga(2, 0, 160, False)
         round_ga(2, 160, 256, True)
         quant_ga(1, 0, 256)
         quant_ga(2, 0, 256)
-        for r in range(PACK):
-            stored_mm(1, r)
-            fresh_mm(1, r)
+        for r0 in (0, 2):
+            for r in (r0, r0 + 1):
+                stored_mm(1, r)
+            for r in (r0, r0 + 1):
+                fresh_mm(1, r)
 
         y = []
         for i, (r0, r1, c0, c1) in enumerate(pieces):

@@ -18,180 +18,201 @@ COPY = mybir.ActivationFunctionType.Copy
 
 P = 128
 PACK = 4
-PASS = P * PACK
+TOKENS = P * PACK
+PASSES = 2
+QUADS = 4
+LINE = 16
+RUN = LINE // 4
+HALF = N // 2
+GRAD_RATE, MOMENTUM = 0.02, 0.5
+
+GA_VECTOR_COLS = 160
+Y_SCALAR_COLS = 104
+
+GA_PIECES = [(0, 0, N), (1, 0, HALF), (1, HALF, N)]
+Y_PIECES = [(0, 1, 0, N), (1, 2, 0, N), (2, 4, 0, HALF), (2, 4, HALF, N)]
 
 
-def tile_mix_wgrad_of_two_stores_pl_kernel(tc, xa, ga, xs_words, xs_scales, gs_words, gs_scales, mom, out_0, out_1, out_2):
+def tile_mix_wgrad_of_two_stores_pl_kernel(
+    tc, xa, ga, xs_words, xs_scales, gs_words, gs_scales, mom, out_0, out_1, out_2
+):
     nc = tc.nc
     with ExitStack() as ctx:
-        sb = ctx.enter_context(tc.tile_pool(name="sb", bufs=1))
+        sbuf = ctx.enter_context(tc.tile_pool(name="sbuf", bufs=1))
         psum = ctx.enter_context(tc.psum_pool(name="psum", bufs=1))
         ctx.enter_context(tc.manual_schedule())
 
         def tile(name, shape, dtype):
-            return sb.tile(shape, dtype, name=name, align_bytes=64)
+            return sbuf.tile(shape, dtype, name=name, align_bytes=64)
 
         acc = [psum.tile([P, N], F32, name="acc%d" % r) for r in range(PACK)]
 
-        xs_raw = tile("xs_raw", [P, 2048], U8)
-        xs_sc_raw = tile("xs_sc_raw", [P, 1024], U8)
-        xs_dealt = tile("xs_dealt", [P, 2048], U8)
-        xs_sc = tile("xs_sc", [P, 1024], U8)
-        gs_codes = [tile("gs_codes%d" % z, [P, N], U32) for z in range(2)]
-        gs_sc = tile("gs_sc", [P, 2 * N], U8)
+        xs_raw = tile("xs_raw", [P, PASSES * K * 2], U8)
+        xs_scales_raw = tile("xs_scales_raw", [P, PASSES * K], U8)
+        xs_dealt = tile("xs_dealt", [P, PASSES * K * 2], U8)
+        xs_scales_dealt = tile("xs_scales_dealt", [P, PASSES * K], U8)
+        gs_codes = [tile("gs_codes%d" % z, [P, N], U32) for z in range(PASSES)]
+        gs_scale_rows = tile("gs_scale_rows", [P, PASSES * N], U8)
 
-        def load_scales(queue, plane, scales, q):
-            queue.dma_start(
-                out=plane[32 * q : 32 * q + 4, :].bitcast(I32).rearrange("p (z c) -> p z c", z=2),
-                in_=scales[:, 4 * q : 4 * q + 4, :].rearrange("z r c -> r z c").bitcast(I32),
-            )
+        def load_scales(queue, dst, scales):
+            for quad in range(QUADS):
+                queue.dma_start(
+                    out=dst[32 * quad : 32 * quad + 4, :].bitcast(I32).rearrange("p (z c) -> p z c", z=PASSES),
+                    in_=scales[:, 4 * quad : 4 * quad + 4, :].rearrange("z q c -> q z c").bitcast(I32),
+                )
 
-        def load_rows(name, src, a, c0, c1):
+        def load_tokens(name, src, a, c0, c1):
             raw = tile(name, [P, PACK, c1 - c0], F32)
-            nc.sync.dma_start(out=raw[:], in_=src[PASS * a : PASS * (a + 1), c0:c1].rearrange("(p j) w -> p j w", j=PACK))
+            rows = src[TOKENS * a : TOKENS * (a + 1), c0:c1]
+            nc.sync.dma_start(out=raw[:], in_=rows.rearrange("(p j) w -> p j w", j=PACK))
             return raw
 
-        nc.vector.memset(xs_sc_raw[:].bitcast(I32), 0)
-        nc.gpsimd.memset(gs_sc[:].bitcast(I32), 0)
+        nc.vector.memset(xs_scales_raw[:].bitcast(I32), 0)
+        nc.gpsimd.memset(gs_scale_rows[:].bitcast(I32), 0)
 
-        ga_cuts = [(0, 0, 512), (1, 0, 256), (1, 256, 512)]
-        gs_v = gs_words.rearrange("z p n t -> z p (n t)").bitcast(I32)
+        gs_view = gs_words.rearrange("z p n j -> z p (n j)").bitcast(I32)
+        mom_view = mom.rearrange("(p r) n -> p r n", r=PACK)
+        out_view = out_0.rearrange("(p r) n -> p r n", r=PACK)
+
         nc.sync.dma_start(
-            out=xs_raw[:].bitcast(I32).rearrange("p (z w) -> p z w", z=2),
+            out=xs_raw[:].bitcast(I32).rearrange("p (z w) -> p z w", z=PASSES),
             in_=xs_words.rearrange("z p b -> p z b").bitcast(I32),
         )
-        xa_raw = [load_rows("xa0", xa, 0, 0, 512)]
-        for q in range(4):
-            load_scales(nc.sync, xs_sc_raw, xs_scales, q)
-        ga_raw = [load_rows("ga0", ga, 0, 0, 512)]
-        for q in range(4):
-            load_scales(nc.gpsimd, gs_sc, gs_scales, q)
-        xa_raw.append(load_rows("xa1", xa, 1, 0, 512))
-        nc.sync.dma_start(out=gs_codes[0][:].bitcast(I32), in_=gs_v[0])
-        ga_raw.append(load_rows("ga1", ga, 1, 0, 256))
-        ga_raw.append(load_rows("ga2", ga, 1, 256, 512))
-        nc.sync.dma_start(out=gs_codes[1][:].bitcast(I32), in_=gs_v[1])
-        mom_v = mom.rearrange("(p r) n -> p r n", r=PACK)
-        out_v = out_0.rearrange("(p r) n -> p r n", r=PACK)
-        pieces = [(0, 1, 0, 512), (1, 2, 0, 512), (2, 4, 0, 256), (2, 4, 256, 512)]
+        xa_raw = [load_tokens("xa_raw0", xa, 0, 0, K)]
+        load_scales(nc.sync, xs_scales_raw, xs_scales)
+        ga_raw = [load_tokens("ga_raw0", ga, *GA_PIECES[0])]
+        load_scales(nc.gpsimd, gs_scale_rows, gs_scales)
+        xa_raw.append(load_tokens("xa_raw1", xa, 1, 0, K))
+        nc.sync.dma_start(out=gs_codes[0][:].bitcast(I32), in_=gs_view[0])
+        ga_raw.append(load_tokens("ga_raw1", ga, *GA_PIECES[1]))
+        ga_raw.append(load_tokens("ga_raw2", ga, *GA_PIECES[2]))
+        nc.sync.dma_start(out=gs_codes[1][:].bitcast(I32), in_=gs_view[1])
         mom_raw = []
-        for i, (r0, r1, c0, c1) in enumerate(pieces):
-            m = tile("mom%d" % i, [P, r1 - r0, c1 - c0], F32)
-            nc.sync.dma_start(out=m[:], in_=mom_v[:, r0:r1, c0:c1])
-            mom_raw.append(m)
+        for i, (r0, r1, c0, c1) in enumerate(Y_PIECES):
+            mom_raw.append(tile("mom_raw%d" % i, [P, r1 - r0, c1 - c0], F32))
+            nc.sync.dma_start(out=mom_raw[i][:], in_=mom_view[:, r0:r1, c0:c1])
 
         nc.vector.tensor_copy(
-            out=xs_dealt[:].rearrange("p (r g m b) -> p g r m b", r=4, m=8, b=2),
-            in_=xs_raw[:].rearrange("p (g m r b) -> p g r m b", r=4, m=8, b=2),
+            out=xs_dealt[:].rearrange("p (r g m b) -> p g r m b", r=PACK, m=LINE // 2, b=2),
+            in_=xs_raw[:].rearrange("p (g m r b) -> p g r m b", r=PACK, m=LINE // 2, b=2),
         )
         nc.vector.tensor_copy(
-            out=xs_sc[:].rearrange("p (r g m) -> p g r m", r=4, m=16),
-            in_=xs_sc_raw[:].rearrange("p (g m r) -> p g r m", r=4, m=16),
+            out=xs_scales_dealt[:].rearrange("p (r g m) -> p g r m", r=PACK, m=LINE),
+            in_=xs_scales_raw[:].rearrange("p (g m r) -> p g r m", r=PACK, m=LINE),
         )
 
-        xa_codes = [tile("xa_codes%d" % a, [P, K], U32) for a in range(2)]
-        xa_sc = [tile("xa_sc%d" % a, [P, K], U8) for a in range(2)]
-        def fresh_xa(a):
-            xa_bf = [tile("xa_bf%d%d" % (a, h), [P, 2 * K], BF16) for h in range(2)]
-            src = xa_raw[a][:].rearrange("p j (m r) -> p m j r", r=4)
-            nc.vector.tensor_copy(out=xa_bf[0][:].rearrange("p (r m j) -> p m j r", r=2, j=4), in_=src[:, :, :, 0:2])
-            nc.scalar.activation(out=xa_bf[1][:].rearrange("p (r m j) -> p m j r", r=2, j=4), in_=src[:, :, :, 2:4], func=COPY)
+        xa_codes = [tile("xa_codes%d" % a, [P, K], U32) for a in range(PASSES)]
+        xa_scale_rows = [tile("xa_scale_rows%d" % a, [P, K], U8) for a in range(PASSES)]
+        ga_codes = [tile("ga_codes%d" % a, [P, N], U32) for a in range(PASSES)]
+        ga_scale_rows = [tile("ga_scale_rows%d" % a, [P, N], U8) for a in range(PASSES)]
+        ga_bf = [tile("ga_bf%d" % i, [P, PACK * (c1 - c0)], BF16) for i, (a, c0, c1) in enumerate(GA_PIECES)]
+
+        def vector_round(dst, src):
+            nc.vector.tensor_copy(out=dst, in_=src)
+
+        def scalar_round(dst, src):
+            nc.scalar.activation(out=dst, in_=src, func=COPY)
+
+        def interleave(round_copy, dst, src, c0, c1):
+            round_copy(
+                dst[:, PACK * c0 : PACK * c1].rearrange("p (c i j) -> p c j i", i=RUN, j=PACK),
+                src[:, :, c0:c1].rearrange("p j (c i) -> p c j i", i=RUN),
+            )
+
+        def quantise_xa(a):
+            src = xa_raw[a][:].rearrange("p j (m r) -> p m j r", r=PACK)
+            xa_bf = [tile("xa_bf%d_%d" % (a, h), [P, 2 * P * PACK], BF16) for h in range(2)]
+            for h, round_copy in enumerate((vector_round, scalar_round)):
+                dst = xa_bf[h][:].rearrange("p (r m j) -> p m j r", r=2, j=PACK)
+                round_copy(dst, src[:, :, :, 2 * h : 2 * h + 2])
             for h in range(2):
-                cols = slice(256 * h, 256 * (h + 1))
-                nc.vector.quantize_mx(out=xa_codes[a][:, cols].bitcast(E4M3), scales=xa_sc[a][:, cols], in_=xa_bf[h][:])
+                cols = slice(2 * P * h, 2 * P * (h + 1))
+                nc.vector.quantize_mx(
+                    out=xa_codes[a][:, cols].bitcast(E4M3), scales=xa_scale_rows[a][:, cols], in_=xa_bf[h][:]
+                )
 
-        def stored_mm(z, r):
-            col = 2 * r + z
+        def quantise_ga(i, c0, c1):
+            a, first = GA_PIECES[i][:2]
+            cols = slice(first + c0, first + c1)
+            nc.vector.quantize_mx(
+                out=ga_codes[a][:, cols].bitcast(E5M2),
+                scales=ga_scale_rows[a][:, cols],
+                in_=ga_bf[i][:, PACK * c0 : PACK * c1],
+            )
+
+        def stored_matmul(z, r):
+            operand = PASSES * r + z
             nc.tensor.matmul_mx(
                 out=acc[r][:],
-                lhsT=xs_dealt[:, 256 * col : 256 * (col + 1)].bitcast(E2M1),
-                lhsT_scale=xs_sc[:, 128 * col : 128 * (col + 1)],
+                lhsT=xs_dealt[:, 2 * P * operand : 2 * P * (operand + 1)].bitcast(E2M1),
+                lhsT_scale=xs_scales_dealt[:, P * operand : P * (operand + 1)],
                 rhs=gs_codes[z][:].bitcast(E4M3),
-                rhs_scale=gs_sc[:, N * z : N * (z + 1)],
+                rhs_scale=gs_scale_rows[:, N * z : N * (z + 1)],
                 start=False,
                 stop=False,
             )
 
-        def fresh_mm(a, r):
+        def fresh_matmul(a, r):
             nc.tensor.matmul_mx(
                 out=acc[r][:],
                 lhsT=xa_codes[a][:, P * r : P * (r + 1)].bitcast(E4M3),
-                lhsT_scale=xa_sc[a][:, P * r : P * (r + 1)],
+                lhsT_scale=xa_scale_rows[a][:, P * r : P * (r + 1)],
                 rhs=ga_codes[a][:].bitcast(E5M2),
-                rhs_scale=ga_sc[a][:],
+                rhs_scale=ga_scale_rows[a][:],
                 start=(a == 0),
-                stop=(a == 1),
+                stop=(a == PASSES - 1),
             )
 
-        ga_codes = [tile("ga_codes%d" % a, [P, N], U32) for a in range(2)]
-        ga_sc = [tile("ga_sc%d" % a, [P, N], U8) for a in range(2)]
-        ga_bf = [tile("ga_bf%d" % i, [P, PACK * (c1 - c0)], BF16) for i, (a, c0, c1) in enumerate(ga_cuts)]
-
-        def round_ga(i, c0, c1, on_scalar):
-            dst = ga_bf[i][:, PACK * c0 : PACK * c1].rearrange("p (c i j) -> p c j i", i=4, j=4)
-            src = ga_raw[i][:, :, c0:c1].rearrange("p j (c i) -> p c j i", i=4)
-            if on_scalar:
-                nc.scalar.activation(out=dst, in_=src, func=COPY)
-            else:
-                nc.vector.tensor_copy(out=dst, in_=src)
-
-        def quant_ga(i, c0, c1):
-            a, base, end = ga_cuts[i]
-            nc.vector.quantize_mx(
-                out=ga_codes[a][:, base + c0 : base + c1].bitcast(E5M2),
-                scales=ga_sc[a][:, base + c0 : base + c1],
-                in_=ga_bf[i][:, PACK * c0 : PACK * c1],
-            )
-
-        fresh_xa(0)
-        round_ga(0, 0, 256, False)
-        round_ga(0, 256, 512, True)
-        quant_ga(0, 0, 256)
-        quant_ga(0, 256, 512)
+        quantise_xa(0)
+        interleave(vector_round, ga_bf[0], ga_raw[0], 0, HALF)
+        interleave(scalar_round, ga_bf[0], ga_raw[0], HALF, N)
+        quantise_ga(0, 0, HALF)
+        quantise_ga(0, HALF, N)
         for r in range(PACK):
-            fresh_mm(0, r)
+            fresh_matmul(0, r)
         for r in range(PACK):
-            stored_mm(0, r)
-        fresh_xa(1)
-        round_ga(1, 0, 256, True)
-        round_ga(2, 0, 160, False)
-        round_ga(2, 160, 256, True)
-        quant_ga(1, 0, 256)
-        quant_ga(2, 0, 256)
-        for r0 in (0, 2):
-            for r in (r0, r0 + 1):
-                stored_mm(1, r)
-            for r in (r0, r0 + 1):
-                fresh_mm(1, r)
+            stored_matmul(0, r)
 
-        y = []
-        for i, (r0, r1, c0, c1) in enumerate(pieces):
-            half = tile("half%d" % i, [P, r1 - r0, c1 - c0], F32)
-            nc.scalar.activation(out=half[:], in_=mom_raw[i][:], func=COPY, scale=0.5)
-            y.append(half)
-        ysb = tile("ysb", [P, PACK, N], F32)
-        for i, (r0, r1, c0, c1) in enumerate(pieces):
+        quantise_xa(1)
+        interleave(scalar_round, ga_bf[1], ga_raw[1], 0, HALF)
+        interleave(vector_round, ga_bf[2], ga_raw[2], 0, GA_VECTOR_COLS)
+        interleave(scalar_round, ga_bf[2], ga_raw[2], GA_VECTOR_COLS, HALF)
+        quantise_ga(1, 0, HALF)
+        quantise_ga(2, 0, HALF)
+        for pair in ((0, 1), (2, 3)):
+            for r in pair:
+                stored_matmul(1, r)
+            for r in pair:
+                fresh_matmul(1, r)
+
+        y = tile("y", [P, PACK, N], F32)
+        for i, (r0, r1, c0, c1) in enumerate(Y_PIECES):
+            mom_scaled = tile("mom_scaled%d" % i, [P, r1 - r0, c1 - c0], F32)
+            nc.scalar.activation(out=mom_scaled[:], in_=mom_raw[i][:], func=COPY, scale=MOMENTUM)
             for r in range(r0, r1):
                 nc.vector.scalar_tensor_tensor(
-                    out=ysb[:, r, c0:c1], in0=acc[r][:, c0:c1], scalar=0.02, in1=y[i][:, r - r0, :], op0=ALU.mult, op1=ALU.add
+                    out=y[:, r, c0:c1],
+                    in0=acc[r][:, c0:c1],
+                    scalar=GRAD_RATE,
+                    in1=mom_scaled[:, r - r0, :],
+                    op0=ALU.mult,
+                    op1=ALU.add,
                 )
-            nc.sync.dma_start(out=out_v[:, r0:r1, c0:c1], in_=ysb[:, r0:r1, c0:c1])
+            nc.sync.dma_start(out=out_view[:, r0:r1, c0:c1], in_=y[:, r0:r1, c0:c1])
 
         y_codes = tile("y_codes", [P, N], U32)
-        y_sc = tile("y_sc", [P, N], U8)
-        y_bf = [tile("y_bf%d" % h, [P, PACK * 256], BF16) for h in range(2)]
-        for h in range(2):
-            dst = y_bf[h][:].rearrange("p (c i r) -> p c r i", i=4, r=4)
-            src = ysb[:, :, 256 * h : 256 * (h + 1)].rearrange("p r (c i) -> p c r i", i=4)
-            if h == 0:
-                nc.scalar.activation(out=dst, in_=src, func=COPY)
-            else:
-                nc.vector.tensor_copy(out=dst, in_=src)
-        words_v = out_1[0].rearrange("p c r -> p (c r)").bitcast(I32)
-        for h in range(2):
-            cols = slice(256 * h, 256 * (h + 1))
-            nc.vector.quantize_mx(out=y_codes[:, cols].bitcast(E4M3), scales=y_sc[:, cols], in_=y_bf[h][:])
-            nc.sync.dma_start(out=words_v[:, cols], in_=y_codes[:, cols].bitcast(I32))
-        for q in range(4):
-            queue = nc.sync if q < 1 else nc.scalar
-            queue.dma_start(out=out_2[0, 4 * q : 4 * q + 4, :].bitcast(I32), in_=y_sc[32 * q : 32 * q + 4, :].bitcast(I32))
+        y_scale_rows = tile("y_scale_rows", [P, N], U8)
+        y_bf = [tile("y_bf%d" % h, [P, PACK * HALF], BF16) for h in range(2)]
+        halves = [slice(HALF * h, HALF * (h + 1)) for h in range(2)]
+        for h, cols in enumerate(halves):
+            interleave(scalar_round, y_bf[h], y[:, :, cols], 0, Y_SCALAR_COLS)
+            interleave(vector_round, y_bf[h], y[:, :, cols], Y_SCALAR_COLS, HALF)
+        words_view = out_1[0].rearrange("p n r -> p (n r)").bitcast(I32)
+        for h, cols in enumerate(halves):
+            nc.vector.quantize_mx(out=y_codes[:, cols].bitcast(E4M3), scales=y_scale_rows[:, cols], in_=y_bf[h][:])
+            nc.sync.dma_start(out=words_view[:, cols], in_=y_codes[:, cols].bitcast(I32))
+        for quad, queue in enumerate((nc.sync, nc.scalar, nc.scalar, nc.scalar)):
+            queue.dma_start(
+                out=out_2[0, 4 * quad : 4 * quad + 4, :].bitcast(I32),
+                in_=y_scale_rows[32 * quad : 32 * quad + 4, :].bitcast(I32),
+            )

from contextlib import ExitStack

import concourse.mybir as mybir

T, S, K, N = 1024, 1024, 512, 512
FLOPS = 2 * (T + S) * K * N

F32 = mybir.dt.float32
BF16 = mybir.dt.bfloat16
I32 = mybir.dt.int32
U32 = mybir.dt.uint32
U8 = mybir.dt.uint8
E4M3 = mybir.dt.float8_e4m3fn_x4
E5M2 = mybir.dt.float8_e5m2_x4
E2M1 = mybir.dt.float4_e2m1fn_x4
ALU = mybir.AluOpType
COPY = mybir.ActivationFunctionType.Copy

P = 128
PACK = 4
TOKENS = P * PACK
PASSES = 2
QUADS = 4
LINE = 16
RUN = LINE // 4
HALF = N // 2
GRAD_RATE, MOMENTUM = 0.02, 0.5

GA_VECTOR_COLS = 160
Y_SCALAR_COLS = 104

GA_PIECES = [(0, 0, N), (1, 0, HALF), (1, HALF, N)]
Y_PIECES = [(0, 1, 0, N), (1, 2, 0, N), (2, 4, 0, HALF), (2, 4, HALF, N)]


def tile_mix_wgrad_of_two_stores_pl_kernel(
    tc, xa, ga, xs_words, xs_scales, gs_words, gs_scales, mom, out_0, out_1, out_2
):
    nc = tc.nc
    with ExitStack() as ctx:
        sbuf = ctx.enter_context(tc.tile_pool(name="sbuf", bufs=1))
        psum = ctx.enter_context(tc.psum_pool(name="psum", bufs=1))
        ctx.enter_context(tc.manual_schedule())

        def tile(name, shape, dtype):
            return sbuf.tile(shape, dtype, name=name, align_bytes=64)

        acc = [psum.tile([P, N], F32, name="acc%d" % r) for r in range(PACK)]

        xs_raw = tile("xs_raw", [P, PASSES * K * 2], U8)
        xs_scales_raw = tile("xs_scales_raw", [P, PASSES * K], U8)
        xs_dealt = tile("xs_dealt", [P, PASSES * K * 2], U8)
        xs_scales_dealt = tile("xs_scales_dealt", [P, PASSES * K], U8)
        gs_codes = [tile("gs_codes%d" % z, [P, N], U32) for z in range(PASSES)]
        gs_scale_rows = tile("gs_scale_rows", [P, PASSES * N], U8)

        def load_scales(queue, dst, scales):
            for quad in range(QUADS):
                queue.dma_start(
                    out=dst[32 * quad : 32 * quad + 4, :].bitcast(I32).rearrange("p (z c) -> p z c", z=PASSES),
                    in_=scales[:, 4 * quad : 4 * quad + 4, :].rearrange("z q c -> q z c").bitcast(I32),
                )

        def load_tokens(name, src, a, c0, c1):
            raw = tile(name, [P, PACK, c1 - c0], F32)
            rows = src[TOKENS * a : TOKENS * (a + 1), c0:c1]
            nc.sync.dma_start(out=raw[:], in_=rows.rearrange("(p j) w -> p j w", j=PACK))
            return raw

        nc.vector.memset(xs_scales_raw[:].bitcast(I32), 0)
        nc.gpsimd.memset(gs_scale_rows[:].bitcast(I32), 0)

        gs_view = gs_words.rearrange("z p n j -> z p (n j)").bitcast(I32)
        mom_view = mom.rearrange("(p r) n -> p r n", r=PACK)
        out_view = out_0.rearrange("(p r) n -> p r n", r=PACK)

        nc.sync.dma_start(
            out=xs_raw[:].bitcast(I32).rearrange("p (z w) -> p z w", z=PASSES),
            in_=xs_words.rearrange("z p b -> p z b").bitcast(I32),
        )
        xa_raw = [load_tokens("xa_raw0", xa, 0, 0, K)]
        load_scales(nc.sync, xs_scales_raw, xs_scales)
        ga_raw = [load_tokens("ga_raw0", ga, *GA_PIECES[0])]
        load_scales(nc.gpsimd, gs_scale_rows, gs_scales)
        xa_raw.append(load_tokens("xa_raw1", xa, 1, 0, K))
        nc.sync.dma_start(out=gs_codes[0][:].bitcast(I32), in_=gs_view[0])
        ga_raw.append(load_tokens("ga_raw1", ga, *GA_PIECES[1]))
        ga_raw.append(load_tokens("ga_raw2", ga, *GA_PIECES[2]))
        nc.sync.dma_start(out=gs_codes[1][:].bitcast(I32), in_=gs_view[1])
        mom_raw = []
        for i, (r0, r1, c0, c1) in enumerate(Y_PIECES):
            mom_raw.append(tile("mom_raw%d" % i, [P, r1 - r0, c1 - c0], F32))
            nc.sync.dma_start(out=mom_raw[i][:], in_=mom_view[:, r0:r1, c0:c1])

        nc.vector.tensor_copy(
            out=xs_dealt[:].rearrange("p (r g m b) -> p g r m b", r=PACK, m=LINE // 2, b=2),
            in_=xs_raw[:].rearrange("p (g m r b) -> p g r m b", r=PACK, m=LINE // 2, b=2),
        )
        nc.vector.tensor_copy(
            out=xs_scales_dealt[:].rearrange("p (r g m) -> p g r m", r=PACK, m=LINE),
            in_=xs_scales_raw[:].rearrange("p (g m r) -> p g r m", r=PACK, m=LINE),
        )

        xa_codes = [tile("xa_codes%d" % a, [P, K], U32) for a in range(PASSES)]
        xa_scale_rows = [tile("xa_scale_rows%d" % a, [P, K], U8) for a in range(PASSES)]
        ga_codes = [tile("ga_codes%d" % a, [P, N], U32) for a in range(PASSES)]
        ga_scale_rows = [tile("ga_scale_rows%d" % a, [P, N], U8) for a in range(PASSES)]
        ga_bf = [tile("ga_bf%d" % i, [P, PACK * (c1 - c0)], BF16) for i, (a, c0, c1) in enumerate(GA_PIECES)]

        def vector_round(dst, src):
            nc.vector.tensor_copy(out=dst, in_=src)

        def scalar_round(dst, src):
            nc.scalar.activation(out=dst, in_=src, func=COPY)

        def interleave(round_copy, dst, src, c0, c1):
            round_copy(
                dst[:, PACK * c0 : PACK * c1].rearrange("p (c i j) -> p c j i", i=RUN, j=PACK),
                src[:, :, c0:c1].rearrange("p j (c i) -> p c j i", i=RUN),
            )

        def quantise_xa(a):
            src = xa_raw[a][:].rearrange("p j (m r) -> p m j r", r=PACK)
            xa_bf = [tile("xa_bf%d_%d" % (a, h), [P, 2 * P * PACK], BF16) for h in range(2)]
            for h, round_copy in enumerate((vector_round, scalar_round)):
                dst = xa_bf[h][:].rearrange("p (r m j) -> p m j r", r=2, j=PACK)
                round_copy(dst, src[:, :, :, 2 * h : 2 * h + 2])
            for h in range(2):
                cols = slice(2 * P * h, 2 * P * (h + 1))
                nc.vector.quantize_mx(
                    out=xa_codes[a][:, cols].bitcast(E4M3), scales=xa_scale_rows[a][:, cols], in_=xa_bf[h][:]
                )

        def quantise_ga(i, c0, c1):
            a, first = GA_PIECES[i][:2]
            cols = slice(first + c0, first + c1)
            nc.vector.quantize_mx(
                out=ga_codes[a][:, cols].bitcast(E5M2),
                scales=ga_scale_rows[a][:, cols],
                in_=ga_bf[i][:, PACK * c0 : PACK * c1],
            )

        def stored_matmul(z, r):
            operand = PASSES * r + z
            nc.tensor.matmul_mx(
                out=acc[r][:],
                lhsT=xs_dealt[:, 2 * P * operand : 2 * P * (operand + 1)].bitcast(E2M1),
                lhsT_scale=xs_scales_dealt[:, P * operand : P * (operand + 1)],
                rhs=gs_codes[z][:].bitcast(E4M3),
                rhs_scale=gs_scale_rows[:, N * z : N * (z + 1)],
                start=False,
                stop=False,
            )

        def fresh_matmul(a, r):
            nc.tensor.matmul_mx(
                out=acc[r][:],
                lhsT=xa_codes[a][:, P * r : P * (r + 1)].bitcast(E4M3),
                lhsT_scale=xa_scale_rows[a][:, P * r : P * (r + 1)],
                rhs=ga_codes[a][:].bitcast(E5M2),
                rhs_scale=ga_scale_rows[a][:],
                start=(a == 0),
                stop=(a == PASSES - 1),
            )

        quantise_xa(0)
        interleave(vector_round, ga_bf[0], ga_raw[0], 0, HALF)
        interleave(scalar_round, ga_bf[0], ga_raw[0], HALF, N)
        quantise_ga(0, 0, HALF)
        quantise_ga(0, HALF, N)
        for r in range(PACK):
            fresh_matmul(0, r)
        for r in range(PACK):
            stored_matmul(0, r)

        quantise_xa(1)
        interleave(scalar_round, ga_bf[1], ga_raw[1], 0, HALF)
        interleave(vector_round, ga_bf[2], ga_raw[2], 0, GA_VECTOR_COLS)
        interleave(scalar_round, ga_bf[2], ga_raw[2], GA_VECTOR_COLS, HALF)
        quantise_ga(1, 0, HALF)
        quantise_ga(2, 0, HALF)
        for pair in ((0, 1), (2, 3)):
            for r in pair:
                stored_matmul(1, r)
            for r in pair:
                fresh_matmul(1, r)

        y = tile("y", [P, PACK, N], F32)
        for i, (r0, r1, c0, c1) in enumerate(Y_PIECES):
            mom_scaled = tile("mom_scaled%d" % i, [P, r1 - r0, c1 - c0], F32)
            nc.scalar.activation(out=mom_scaled[:], in_=mom_raw[i][:], func=COPY, scale=MOMENTUM)
            for r in range(r0, r1):
                nc.vector.scalar_tensor_tensor(
                    out=y[:, r, c0:c1],
                    in0=acc[r][:, c0:c1],
                    scalar=GRAD_RATE,
                    in1=mom_scaled[:, r - r0, :],
                    op0=ALU.mult,
                    op1=ALU.add,
                )
            nc.sync.dma_start(out=out_view[:, r0:r1, c0:c1], in_=y[:, r0:r1, c0:c1])

        y_codes = tile("y_codes", [P, N], U32)
        y_scale_rows = tile("y_scale_rows", [P, N], U8)
        y_bf = [tile("y_bf%d" % h, [P, PACK * HALF], BF16) for h in range(2)]
        halves = [slice(HALF * h, HALF * (h + 1)) for h in range(2)]
        for h, cols in enumerate(halves):
            interleave(scalar_round, y_bf[h], y[:, :, cols], 0, Y_SCALAR_COLS)
            interleave(vector_round, y_bf[h], y[:, :, cols], Y_SCALAR_COLS, HALF)
        words_view = out_1[0].rearrange("p n r -> p (n r)").bitcast(I32)
        for h, cols in enumerate(halves):
            nc.vector.quantize_mx(out=y_codes[:, cols].bitcast(E4M3), scales=y_scale_rows[:, cols], in_=y_bf[h][:])
            nc.sync.dma_start(out=words_view[:, cols], in_=y_codes[:, cols].bitcast(I32))
        for quad, queue in enumerate((nc.sync, nc.scalar, nc.scalar, nc.scalar)):
            queue.dma_start(
                out=out_2[0, 4 * quad : 4 * quad + 4, :].bitcast(I32),
                in_=y_scale_rows[32 * quad : 32 * quad + 4, :].bitcast(I32),
            )
